import numpy as np, ml_dtypes
CORES = [35,38,43,46]
N = 4
BF = ml_dtypes.bfloat16
V, NT, A, S, RO, CAP, VO, L = 4096, 128, 6, 8, 2, 64, 1024, 256
def parts(rng):
    par = np.zeros((N, 8, 16, NT), np.int64)
    for j in range(1, A): par[:, :, j] = rng.integers(0, j, (N, 8, NT))
    share = rng.choice(np.array([0.0, 0.3, 0.5, 0.7, 1.0]), (N, 8, 1, NT))
    return {"x": rng.integers(0, 256, (N, 8, 16, V)), "nb": rng.integers(0, V, (N, 8, 16, V)), "feat": rng.integers(0, 256, (N, 8, 16, (A - 1) * NT)), "chg": rng.integers(0, 256, (N, 8, 16, A * NT)),
            "par": par, "swp": (rng.random((N, 8, 16, NT)) < share).astype(np.int64), "wt": rng.integers(0, 64, (N, 8, 16, 1)), "beg": rng.integers(0, V, (N, 8, L)), "tau": rng.integers(0, NT, (N, 8, L))}
def limits(rng, p):
    base = np.array([650, 800, 950, 1100])[(np.arange(8)[None, :] + rng.integers(0, 4, (N, 1))) % 4]
    p["par"][:, :, 9:8 + A] = base[:, :, None, None] + rng.integers(0, 400, (N, 8, A - 1, NT))
    return p
def spell(rng, d):
    a = (d[None, :] + rng.permuted(np.tile(np.arange(16)[:, None], (1, V)), axis=0)) // 16
    t = np.floor(rng.random((8, V)) * (np.minimum(a[::2], 255 - a[1::2]) + 1)).astype(np.int64)
    a[::2] -= t; a[1::2] += t
    return a
def pack(p):
    o = {}
    for k in ("x", "nb", "feat", "chg", "par", "swp", "wt"):
        a = np.ascontiguousarray(p[k]).reshape(N, 128, -1)
        o[k] = a.astype(np.float32).astype(BF) if k in ("x", "feat", "chg", "swp") else a.astype(np.int32)
    o["beg"] = p["beg"].astype(np.int32); o["tau"] = p["tau"].astype(np.int32)
    return o
def setup_inputs(rng):
    return pack(limits(rng, parts(rng)))
def setup_inputs_brim(rng):
    p = parts(rng); p["x"] = np.minimum(p["x"], 254); h = V // 16
    for q in range(N):
        for g in range(8): p["nb"][q, g] = rng.permutation(16)[:, None] * h + rng.integers(0, h, (16, V))
    p["par"][:, :, 9:8 + A] = 4080; odd = np.arange(1, NT, 2); f = rng.integers(1, A, NT // 2)
    p["par"][:, :, 8 + f, odd] = 0; p["feat"][:, :, :, (f - 1) * NT + odd] = 255
    for q in range(N):
        for g in range(8):
            n = int(rng.choice(np.array([0, 1, CAP - 1, CAP, CAP + 1, L])))
            if q == 0: n = (CAP, CAP + 1, L, CAP - 1, 1, 0, CAP, CAP + 1)[g]
            if q == 1 and g < 2: n = CAP
            t = 2 * rng.integers(0, NT // 2, L); t[rng.permutation(L)[n:]] += 1; p["tau"][q, g] = t
    return pack(p)
def setup_inputs_clash(rng):
    p = parts(rng); p["par"][:, :, 9:8 + A] = rng.choice(np.array([4080, 1300]), (N, 8, 1, NT))
    for q in range(N):
        few = rng.permutation(V)[:64]; few[0] = 0; few[1] = V - 1
        p["nb"][q, 0] = few[rng.integers(0, 64, (16, V))]; p["beg"][q, 0] = few[rng.integers(0, 64, L)]
        a = p["tau"][q, 0, 0]; p["beg"][q, 0, 0] = V - 1; p["par"][q, 0, 9:8 + A, a] = 4080; p["swp"][q, 0, :, a] = 1
        p["nb"][q, 1] = p["nb"][q, 1, :1]
        for g in (2, 6): p["nb"][q, g] = np.where(rng.random((16, V)) < 0.5, np.arange(V)[None, :], p["nb"][q, g])
        s = rng.integers(0, V, 24); s[0] = 0; s[1] = V - 1; p["beg"][q, 3] = s[rng.integers(0, 24, L)]
        p["nb"][q, 4] = (V // 8) * rng.integers(0, 8, (16, V)); p["beg"][q, 4] = (V // 8) * rng.integers(0, 8, L)
        for g in (5, 7):
            o = rng.permutation(V); p["nb"][q, g, 0, o] = np.roll(o, -1)
            p["par"][q, g, 1:A] = np.arange(A - 1)[:, None]; p["par"][q, g, 9:8 + A] = 4080
            if g == 5:
                n = 256 // A; s = rng.integers(0, A, L); s[:n] = 0; s[n] = A - 256 % A; s[n + 1] = 0
                p["tau"][q, g] = int(p["tau"][q, g, 0])
            else: s = A * np.arange(L)
            p["beg"][q, g] = o[s % V]
    return pack(p)
def setup_inputs_ties(rng):
    p = parts(rng); p["x"] = rng.integers(0, 4, p["x"].shape); p["feat"] = rng.integers(0, 4, p["feat"].shape)
    p["chg"] = rng.choice(np.array([0, 1, 2, 255]), p["chg"].shape)
    p["par"][:, :, 9:8 + A] = rng.integers(12, 22, (N, 8, A - 1, NT))
    for q in range(N):
        two = rng.integers(0, 256, (16, 2)); p["x"][q, 1] = two[:, rng.integers(0, 2, V)]; p["feat"][q, 1] = two[:, rng.integers(0, 2, (A - 1) * NT)]
        p["par"][q, 1, 9:8 + A] = rng.choice(np.array([4080, 0]), (A - 1, NT))
        p["nb"][q, 1] = np.where(rng.random((16, V)) < 0.5, np.arange(V)[None, :], p["nb"][q, 1])
        for g, e in ((3, (2048, 2049, 2050, 2051, 2052)), (5, (3839, 3840, 3841, 3900, 4078, 4079, 4080))):
            t = np.array(e); s = spell(rng, np.minimum(t[rng.integers(0, len(e), V)] + rng.integers(-1, 2, V), 4080))
            m = rng.integers(0, 2 if g == 3 else 1, (16, 1))
            p["x"][q, g] = np.where(m == 1, 255 - s, s); p["feat"][q, g] = 255 * m
            p["par"][q, g, 9:8 + A] = t[rng.integers(0, len(e), (A - 1, NT))]
        p["wt"][q, 5] = rng.integers(60, 64, (16, 1))
    return pack(p)
def setup_inputs_walk(rng):
    p = limits(rng, parts(rng))
    for q in range(N):
        for g in range(0, 8, 2):
            v = np.zeros((A, NT), np.int64); v[0] = rng.integers(0, V, NT); v[0, 0] = 0; v[0, 1] = V - 1; a = np.arange(NT)
            for j in range(1, A):
                k = rng.integers(0, 16, NT); e = rng.random(NT); k = np.where(e < 0.25, 0, np.where(e < 0.5, 15, k))
                v[j] = p["nb"][q, g][k, v[p["par"][q, g, j], a]]
                p["feat"][q, g, :, (j - 1) * NT:j * NT] = p["x"][q, g][:, v[j]]; p["par"][q, g, 8 + j] = 0
            t = rng.permutation(np.arange(L) % NT); p["tau"][q, g] = t
            p["beg"][q, g] = np.where(rng.random(L) < 0.3, rng.integers(0, V, L), v[0][t])
    return pack(p)
def setup_inputs_spread(rng):
    p = parts(rng)
    for k in ("x", "feat", "chg"):
        s = p[k].shape; p[k] = np.floor(np.exp2(8 * rng.random((N, 8, 1, s[3]))) * rng.random(s)).astype(np.int64)
    e = rng.permuted(np.tile(np.array([0.5, 0.5, 1.0, 1.0, 2.0, 2.0, 4.0, 4.0]), (N, 1)), axis=1)
    p["par"][:, :, 9:8 + A] = np.minimum(np.floor(4081 * rng.random((N, 8, A - 1, NT)) ** e[:, :, None, None]), 4080).astype(np.int64)
    p["nb"] = np.floor(V * rng.random(p["nb"].shape) ** 2).astype(np.int64); p["beg"] = np.floor(V * rng.random((N, 8, L)) ** 3).astype(np.int64)
    p["wt"] = np.floor(np.exp2(6 * rng.random((N, 8, 16, 1))) * (0.5 + 0.5 * rng.random((N, 8, 16, 1)))).astype(np.int64)
    return pack(p)
def check_inputs(d):
    bad = []
    def test(k, a, lo, hi):
        a = np.asarray(a).astype(np.float64)
        if not (np.all(a >= lo) and np.all(a <= hi) and np.all(a == np.floor(a))): bad.append("range of " + k)
    for k, hi in (("x", 255), ("nb", V - 1), ("feat", 255), ("chg", 255), ("swp", 1), ("wt", 63), ("beg", V - 1), ("tau", NT - 1)): test(k, d[k], 0, hi)
    p = np.asarray(d["par"]).reshape(N, 8, 16, NT); rest = list(range(16))
    for j in range(1, A):
        test("parents in par", p[:, :, j], 0, j - 1); test("thresholds in par", p[:, :, 8 + j], 0, 4080); rest.remove(j); rest.remove(8 + j)
    test("other rows of par", p[:, :, rest], 0, 0)
    return bad
def reference(x, nb, feat, chg, par, swp, wt, beg, tau):
    B = N * 8; b = np.arange(B)[:, None]; b3 = b[:, :, None]; lane = np.arange(L); li = lane[None, :]
    def items(a, ty): return np.array(a.astype(np.float32).reshape(B, 16, -1).transpose(0, 2, 1), dtype=ty, order="C")
    X = items(x, np.int16); NB = items(nb, np.int32); F = items(feat, np.int16); C = items(chg, np.int16); P = items(par, np.int64); H = items(swp, np.int64) == 1
    W = wt.astype(np.int64).reshape(B, 1, 16); m0 = beg.astype(np.int64).reshape(B, L); T = tau.astype(np.int64).reshape(B, L)
    for rnd in range(RO):
        M = np.full((B, L, A), -1, np.int64); M[:, :, 0] = m0; K = np.zeros((B, L, A), np.int64); j = np.ones((B, L), np.int64)
        for step in range(S):
            jj = np.minimum(j, A - 1)
            c = NB[b, M[b, li, P[b, T, jj]]]
            dist = np.add.reduce(np.abs(X[b3, c] - F[b, (jj - 1) * NT + T][:, :, None, :]), axis=3, dtype=np.int32)
            good = (dist <= P[b, T, 8 + jj][:, :, None]) & (np.arange(16) >= K[b, li, jj][:, :, None])
            for i in range(A - 1): good &= (c != M[:, :, i:i + 1]) | (i >= jj)[:, :, None]
            found = np.any(good, axis=2); k = np.argmax(good, axis=2); ck = np.take_along_axis(c, k[:, :, None], 2)[:, :, 0]
            up = (j < A) & found; down = (j < A) & ~found
            bb, ll = np.nonzero(up); M[bb, ll, j[up]] = ck[up]; K[bb, ll, j[up]] = k[up] + 1
            j = np.where(up, j + 1, np.where(down, np.maximum(j - 1, 1), j))
            fresh = up & (j < A); bb, ll = np.nonzero(fresh); K[bb, ll, j[fresh]] = 0
        full = j == A; slot = np.argsort(~full, axis=1, kind="stable")[:, :CAP]
        got = np.take_along_axis(full, slot, 1); Ms = M[b, slot]; Ts = T[b, slot]
        same = np.any(Ms[:, :, None, :, None] == Ms[:, None, :, None, :], axis=(3, 4))
        lower = np.arange(CAP)[None, :] < np.arange(CAP)[:, None]
        go = got & ~np.any(same & lower & got[:, None, :], axis=2)
        bb, ss = np.nonzero(go); mm = Ms[bb, ss]; tt = Ts[bb, ss]; h = H[bb, tt]
        for i in range(0, A - 1, 2):
            p = NB[bb, mm[:, i]]; q = NB[bb, mm[:, i + 1]]
            NB[bb, mm[:, i]] = np.where(h, q, p); NB[bb, mm[:, i + 1]] = np.where(h, p, q)
        new = (X[bb[:, None], mm] + C[bb[:, None], np.arange(A)[None, :] * NT + tt[:, None]]) & 255
        X[bb[:, None], mm] = new
        Z = np.zeros((B, CAP, 16), np.int16); Z[bb, ss] = np.maximum.reduce(new, axis=1)
        Zr = Z.reshape(N, 8, CAP, 16); t = np.arange(CAP)
        come = np.stack([Zr[(r - 1 - t % (N - 1)) % N, :, t].transpose(1, 0, 2) for r in range(N)])
        u = np.add.reduce(X[b, M[b, li, j - 1]].astype(np.int64) * W, axis=2)
        u[:, :CAP] = np.add.reduce(come.reshape(B, CAP, 16).astype(np.int64) * W, axis=2)
        u = u & 4095
        T = (((u * u) >> 5) + li) & (NT - 1); m0 = (37 * u + li) & (V - 1)
    ym = np.where(np.arange(A)[None, None, :] < j[:, :, None], M, -1).transpose(0, 2, 1).reshape(N, 8, A * L)
    yx = X[:, :VO].transpose(0, 2, 1).reshape(N, 128, VO); yz = come.transpose(0, 1, 3, 2).reshape(N, 128, CAP)
    return {"yx": yx.astype(np.float32).astype(BF), "ym": ym.astype(np.float32), "yz": yz.astype(np.float32).astype(BF)}

import numpy as np
from concourse.bass import DstId, RemoteDMATransfer
from concourse.mybir import AluOpType, ActivationFunctionType

S = np.s_
F32, BF, F16, I32, U16 = "float32", "bfloat16", "float16", "int32", "uint16"
SIZE = {F32: 4, BF: 2, F16: 2, I32: 4, U16: 2}
NV = 4096
NSLOT = [0, 1, 2, 3, 4, 4, 3]
POOL = [None, "a", "b", "c", "d", "e", "c"]
A18 = float(2 ** 18)
C36 = 1.5 * 2.0 ** 36
C41 = 1.5 * 2.0 ** 41
TOP = 126976.0
CH = [(0, 64), (64, 128)]
POS = [0, 3, 1, 4, 2, 5]
WG = 6.0
OFF = {'txg8xw': -2.3, 'tpd14zall': -6.3, 'tfb0tfa': 4.6, 'tof0pd': 6.9, 'tpv4st': -2.5, 'tof0pf': 1.5, 'tal0pd': 4.4,
       'tfl2pv': -5.6, 'tpd0v16': -3.0, 'teq0pd': 2.3, 'tpv0tb': -2.4, 'tmx4xg': 2.3, 'tpv0r': -5.0, 'tmx14xg': -2.2,
       'tpv0inb': -4.0, 'cpf3w2': -3.2, 'tpv0xg': 4.3, 'cr160pf': 0.7, 'cpv4rm': -0.8, 'tO3keep': 0.4, 'tbr1O': -1.1}


def pw(n):
    return 16 * n + 16


LOG = {}
IO = {"x": ([128, 4096], BF), "nb": ([128, 4096], I32), "feat": ([128, 640], BF), "chg": ([128, 768], BF),
      "par": ([128, 128], I32), "swp": ([128, 128], BF), "wt": ([128, 1], I32), "beg": ([8, 256], I32),
      "tau": ([8, 256], I32), "yx": ([128, 1024], BF), "ym": ([8, 1536], F32), "yz": ([128, 64], BF),
      "snt0": ([1, 1], BF), "snt1": ([1, 1], BF)}


def A(name, idx=None):
    return ("ap", name, S[:] if idx is None else idx)


def ind(win, off):
    return ("ind", win, off)


def info(name):
    if name in IO:
        return "dram", IO[name][0], IO[name][1]
    return LOG[name]


def span(ap):
    where, shape, dt = info(ap[1])
    idx = ap[2] if isinstance(ap[2], tuple) else (ap[2],)
    n = int(np.prod(shape[1:]))
    if where == "dram":
        return where, ap[1], 0, 1, n, 1
    cols = np.arange(n).reshape(shape[1:])[idx[1:]] if len(idx) > 1 else np.arange(n)
    m = np.zeros(n, np.uint8)
    m[cols.ravel()] = 1
    return (where, ap[1], int(cols.min()) * SIZE[dt], (int(cols.max()) + 1) * SIZE[dt], int(cols.size),
            int.from_bytes(np.packbits(m).tobytes(), "big"))


OPS = []
GRP = [0, "s"]
CYC, PCYC, GRATE, SRATE = 1.04e-3, 0.52e-3, 1.56, 3.8


def flat(aps):
    o = []
    for a in aps:
        if isinstance(a, tuple):
            o += [a[1], a[2]] if a[0] == "ind" else [a]
    return o


def group(kind):
    GRP[:] = [GRP[0] + 1, kind]


def add(eng, kind, out, ins, cost, **kw):
    w = out[1] if out[0] == "ind" else out
    r = [span(a) for a in flat(ins) + ([out[2]] if out[0] == "ind" else [])]
    sw = span(w)
    cls = "%s%s%d%s" % (GRP[1], w[1].rstrip("01"), sw[2] // 256, r[0][1].rstrip("01") if r else "")
    OPS.append(dict(grp=GRP[0], cls=cls, eng=eng, kind=kind, out=out, ins=ins, cost=cost, w=[sw], r=r, **kw))


def vcost(out, ins, two=False, eng="v"):
    fix = 0.05 if eng == "v" else 0.065
    if out[0] == "ind":
        return fix + 16 * span(out[2])[4] * SRATE * CYC
    if ins and ins[0][0] == "ind":
        return fix + 16 * span(ins[0][2])[4] * GRATE * CYC
    n = span(out)[4]
    f = 1.0
    if eng == "v" and all(SIZE[info(a[1])[2]] == 2 for a in [out] + ins if span(a)[4] == n):
        f = 0.5
    if two:
        f = 2.0 if all(info(a[1])[0] == "sbuf" for a in ins) else 1.0
    return max(64, n * f) * CYC + 0.02


def mm(out, lhsT, rhs, start=True, stop=True):
    add("t", "mm", out, [lhsT, rhs], max(min(64, span(lhsT)[4]), span(rhs)[4]) * PCYC, start=start, stop=stop)


def tr(out, in_, ident):
    add("t", "tr", out, [in_, ident], 4 * 128 * PCYC)


def cp(out, in_):
    add("v", "cp", out, [in_], vcost(out, [in_]))


def tt(out, a, b, op):
    add("v", "tt", out, [a, b], vcost(out, [a, b], True), op=op)


def ts(out, a, s1, op0, s2=None, op1=None):
    add("v", "ts", out, [a, s1, s2], vcost(out, [a]), op0=op0, op1=op1)


def scan(out, d0, d1, init, op0, op1):
    add("v", "scan", out, [d0, d1, init], vcost(out, [d0, d1]), op0=op0, op1=op1)


def ms(out, val):
    add("v", "ms", out, [], vcost(out, []), val=val)


def act(out, in_):
    add("s", "act", out, [in_], vcost(out, [in_], eng="s"))


def scale(out, in_, c, kind="act"):
    add("s", kind, out, [in_, c], vcost(out, [in_], eng="s"))


def iota(out, pattern, base, cm):
    add("g", "iota", out, [], 0.13 + 2 * span(out)[4] * CYC, pattern=pattern, base=base, cm=cm)


def fill(ap, val, step=0):
    iota(ap, [[step, span(ap)[4]]], int(val), 0)


def dma(eng, out, in_, nbytes):
    add(eng, "dma", out, [in_], 0.1, lat=2.0 + nbytes / 180e3)


def to_w(out, z, rhs_of, first=True):
    for a in range(16):
        mm(out, A(z, S[:, 15 - a:143 - a]), rhs_of(a), first and a == 0, a == 15)


CN = ["lo2", "sinit", "bmax", "cc", "ed", "wmp", "wf", "we0", "we1", "we2", "we3", "we4", "wtf", "pre", "wpar", "tfd",
      "tf1", "tf2", "tf3", "tf4", "tf5", "w2"]


def col(name):
    k = 16 * CN.index(name) + 15
    return A("wc", S[:, k:k + 1])


def columns():
    def W(name, r0, r1):
        k = 16 * CN.index(name)
        return A("wv", S[:, k + r0:k + r1])
    ms(A("wv"), 0.0)
    k = 16 * CN.index("we0")
    fill(A("wv", S[:, k:k + 80:17]), 1)
    k = 16 * CN.index("tf1")
    fill(A("wv", S[:, k + 2:k + 80:16]), 1, 1)
    fill(A("wv", S[:, k - 13:k + 80:16]), 1)
    fill(W("lo2", 0, 6), -1, 64)
    fill(W("ed", 6, 10), 1, 1)
    fill(W("ed", 10, 15), 0, 1)
    fill(W("wf", 11, 15), 128, 128)
    for name, r0, r1, v in (("lo2", 6, 16, -1), ("sinit", 0, 10, 2 ** 22), ("sinit", 10, 15, 1), ("bmax", 0, 10, -4096),
                            ("bmax", 10, 16, 8192), ("cc", 0, 6, 2.0 ** 60), ("cc", 6, 15, C41), ("cc", 15, 16, 2.0 ** 60),
                            ("wmp", 6, 10, 1), ("wmp", 11, 15, 2048), ("wf", 15, 16, 1), ("we1", 10, 11, 16384),
                            ("we2", 10, 12, 16384), ("we3", 10, 13, 16384), ("we4", 10, 14, 16384), ("wtf", 0, 1, 2.0 ** 29),
                            ("wtf", 1, 4, 2.0 ** 21), ("pre", 0, 6, 4000), ("wpar", 2, 6, 2 * A18), ("tfd", 1, 2, -1)):
        ms(W(name, r0, r1), float(v))
    ms(W("wtf", 2, 3), 0.0)
    iota(A("r16s"), [[0, len(CN)], [1, 16]], 0, 0)
    ts(A("ohr"), A("r16s"), A("pf", S[:, 0:1]), "is_equal")
    ts(A("r16s"), A("r16s"), 0.0, "not_equal")
    scan(W("w2", 0, 16), A("half"), A("zero"), 65536.0, "mult", "add")
    tt(A("wv"), A("wv"), A("ohr"), "mult")
    scan(A("wc"), A("r16s"), A("wv"), 0.0, "mult", "add")


def setup():
    dma("y", A("bt", S[0:8, 0:256]), A("beg"), 8192)
    dma("s", A("bt", S[0:8, 256:512]), A("tau"), 8192)
    dma("y", A("pari"), A("par"), 65536)
    dma("s", A("tfa", S[:, 640:768]), A("feat", S[:, 0:128]), 32768)
    dma("y", A("nbw", S[:, 0:2048]), A("nb", S[:, 0:2048]), 2 ** 21)
    dma("s", A("nbw", S[:, 2048:4096]), A("nb", S[:, 2048:4096]), 2 ** 21)
    dma("y", A("xw", S[:, 0:4096]), A("x"), 3 * 2 ** 20)
    dma("y", A("tfa", S[:, 128:640]), A("feat", S[:, 128:640]), 3 * 2 ** 20)
    dma("y", A("chw"), A("chg"), 3 * 2 ** 20)
    dma("y", A("sww"), A("swp"), 3 * 2 ** 20)
    dma("y", A("wti", S[:, 0:1]), A("wt"), 3 * 2 ** 20)
    iota(A("pi", S[:, 0:1]), [[0, 1]], 0, 1)
    iota(A("n144"), [[1, 144]], 0, 0)
    iota(A("z8f"), [[1, 144]], 0, -16)
    iota(A("nmp"), [[1, 128]], 0, -1)
    iota(A("n16"), [[16, 8], [0, 16]], 0, 0)
    iota(A("kpat"), [[0, 8], [-8192, 16]], 15 * 8192, 0)
    ts(A("pi", S[:, 1:2]), A("pi", S[:, 0:1]), 15, "bitwise_and")
    ts(A("pi", S[:, 2:3]), A("pi", S[:, 0:1]), 112, "bitwise_and")
    cp(A("pf", S[:, 0:2]), A("pi", S[:, 1:3]))
    rcol, gcol = A("pf", S[:, 0:1]), A("pf", S[:, 1:2])
    ts(A("z8"), A("z8f"), 15.0, "is_equal")
    ts(A("bt16", S[0:8, 0:256]), A("bt", S[0:8, 0:256]), 2048.0, "subtract")
    cp(A("bt16", S[0:8, 256:512]), A("bt", S[0:8, 256:512]))
    ms(A("half"), 0.5)
    ms(A("zero"), 0.0)
    columns()
    ts(A("pf", S[:, 2:3]), col("ed"), A18, "mult", col("cc"), "add")
    ts(A("pf", S[:, 3:4]), rcol, A18, "mult", C41, "add")
    ts(A("pf", S[:, 4:5]), rcol, A18, "mult", -4096.0, "add")
    ts(A("pf", S[:, 5:6]), col("lo2"), 8192.0, "mult")
    ts(A("pf", S[:, 6:7]), rcol, 24.0, "mult", 4096.0, "add")
    ms(A("pf", S[:, 7:8]), -255.5)
    ms(A("pf", S[:, 8:9]), -128.0)
    ts(A("zf"), A("n144"), gcol, "subtract", 15.0, "is_equal")
    ts(A("bo"), A("n16"), gcol, "is_equal")
    ts(A("oh"), A("n144", S[:, 0:16]), rcol, "is_equal")
    ts(A("i32"), A("nmp"), 0.0, "is_equal")
    ts(A("ish"), A("nmp"), 4.0, "is_equal", col("wpar"), "mult")
    act(A("ibf"), A("i32"))
    scale(A("i128"), A("i32"), -128.0)
    scale(A("inb"), A("i32"), -2.0 ** 35)
    for i in range(5):
        scale(A("ni5", S[:, i * 128:(i + 1) * 128]), A("i32"), -1.0)
        scale(A("e5", S[:, i * 128:(i + 1) * 128]), A("bo"), col("we%d" % i))
    for a in range(16):
        scale(A("rm", S[:, a, :]), A("bo"), A("oh", S[:, a:a + 1]))
    scale(A("rmn"), A("rm", S[:, 10, :]), -1.0)
    scale(A("zmp"), A("zf"), col("wmp"))
    scale(A("zfi"), A("zf"), col("wf"))
    scale(A("z0"), A("zf"), A("oh", S[:, 0:1]))
    scale(A("z15"), A("zf"), A("oh", S[:, 15:16]))
    act(A("zall"), A("zf"))
    scale(A("rt"), A("bo"), col("wtf"))
    scale(A("r8", S[:, 0:8]), A("bo", S[:, 0:128:16]), 2.0 ** 21)
    scale(A("r8", S[:, 8:16]), A("bo", S[:, 0:128:16]), -2.0 ** 22)
    scale(A("rf"), A("bo"), 2.0 ** 21)
    tt(A("kpat"), A("kpat"), A("bo"), "mult")
    scale(A("kp2"), A("kpat"), A("oh", S[:, 3:4]))
    ts(A("n16"), A("bo"), A("oh", S[:, 2:3]), "mult", A18, "mult")
    tt(A("rk"), A("kp2"), A("n16"), "add")
    scale(A("w2"), A("bo"), col("w2"))
    scale(A("w16"), A("bo"), 65536.0)
    ts(A("hli", S[:, 0:128]), A("pari"), 8, "arith_shift_right")
    ts(A("hli", S[:, 128:256]), A("pari"), 255, "bitwise_and")
    cp(A("hl"), A("hli"))
    fill(A("tfa", S[:, 0:128]), 0)
    fill(A("ones"), 1)
    scale(A("tfb", S[:, 0:128]), A("ones", S[:, 0:128]), col("tfd"))
    for j in (1, 2, 3, 4, 5):
        scale(A("zs", S[:, j - 1, :]), A("zf"), A("oh", S[:, 8 + j:9 + j]))
        o = A("pf%d" % (j % 2), S[:, (j // 2) * 128:(j // 2 + 1) * 128])
        mm(o, A("zs", S[:, j - 1, 15:143]), A("hl", S[:, 0:128]), True, False)
        mm(o, A("zs", S[:, j - 1, 14:142]), A("hl", S[:, 128:256]), False, True)
        c0 = 640 if j == 1 else (j - 1) * 128
        ts(A("tfb", S[:, c0:c0 + 128]), o, col("tf%d" % j), "add")
    mm(A("pv1", S[:, 0:128]), A("ish"), A("hl", S[:, 128:256]))
    ts(A("ptab"), A("pv1", S[:, 0:128]), A("pf", S[:, 5:6]), "add")
    ts(A("stab"), A("n144", S[:, 0:128]), A("oh", S[:, 15:16]), "mult", col("sinit"), "add")
    ts(A("lw"), A("n144", S[:, 0:16]), 16.0, "mult", rcol, "add")
    ts(A("lw16"), A("lw"), 256.0, "add")
    ts(A("dumt"), A("n144", S[:, 0:24]), A("pf", S[:, 6:7]), "add")
    iota(A("i6"), [[128, 2], [256, 3]], 0, 0)
    for n in (1, 2, 3, 4):
        fill(A("keep%d" % n), 1)
        fill(A("keep%d" % n, S[:, 0:2 * pw(n):pw(n)]), 0)
    for m in range(1, 6):
        for s in (0, 1):
            p, n = "P%s%d" % (POOL[m], s), NSLOT[m]
            iota(A(p, S[:, :, 0:2 * pw(n):pw(n)]), [[0, 4], [0, 2]], 8192, 0)
            for h in (1, 2):
                iota(A(p, S[:, :, h * pw(n) - 15:h * pw(n)]), [[0, 4], [0, 15]], 0, 0)
    fill(A("xw", S[:, NV:NV + 384]), 0)
    fill(A("nbw", S[:, NV:NV + 384]), 0)
    for tl in range(16):
        iota(A("thc", S[:, tl:64:16, :]), [[0, 4], [0, 6]], -2 ** (16 - tl), 0)
    cp(A("wtf32", S[:, 0:1]), A("wti", S[:, 0:1]))
    scale(A("zw"), A("zf"), A("wtf32", S[:, 0:1]))
    for a in range(16):
        mm(A("pd0", S[:, 0:32]), A("z8", S[0:8, 15 - a:143 - a]), A("bt16", S[0:8, a:512:16]), a == 0, a == 15)
    for s in (0, 1):
        ts(A("m0w%d" % s), A("pd0", S[:, 8 * s:8 * s + 8]), 2048.0, "add")
        cp(A("qw%d" % s), A("pd0", S[:, 16 + 8 * s:24 + 8 * s]))


def state(s, B, old, last):
    pv, st = "pv%d" % s, A("st%d" % s)
    X, H, G = A(pv, S[:, 128:256]), A(pv, S[:, 256:384]), A(pv, S[:, 384:512])
    sc = A("sca", S[:, 128 * s:128 * s + 128])
    tt(A("r1%d" % s), old, B, "min")
    tt(X, A("l2%d" % s), B, "subtract")
    if last == 1:
        ts(G, B, C41, "add", A("pf", S[:, 3:4]), "is_equal")
    elif last == 0:
        ts(G, B, col("cc"), "add", A("pf", S[:, 2:3]), "is_equal")
    tt(st, A("r1%d" % s), X, "max")
    ts(H, st, C36, "add", C36, "subtract")
    tt(sc, st, H, "subtract")
    if last != 2:
        tt(A("v16%d" % s), sc, G, "mult")


def begin(s):
    of, pb, bf = "of%d" % s, "pd%d" % s, A("pv%d" % s, S[:, 0:128])
    cp(A(of, S[:, 0:8]), A("m0w%d" % s))
    ts(A(of, S[:, 8:16]), A("qw%d" % s), 640.0, "add")
    cp(A(of, S[:, 16:24]), A("qw%d" % s))
    ts(A("m16%d" % s), A("m0w%d" % s), 2048.0, "subtract")
    for a in range(16):
        mm(A(pb, S[:, 768 + a:896:16]), A("rm", S[:, a, :]), A("m16%d" % s))
    ts(bf, A(pb, S[:, 768:896]), col("bmax"), "max")
    act(A("l2%d" % s), ind(A("ptab"), A(of, S[:, 16:24])))
    act(A("si%d" % s), ind(A("stab"), A(of, S[:, 16:24])))
    state(s, bf, A("si%d" % s), 0)


def turn(rnd, m, s):
    of, cu, c16, fb, tb = ["%s%d" % (n, s) for n in ("of", "cu", "c16", "fb", "tb")]
    xg, mx, pf, pv, pd = ["%s%d" % (n, s) for n in ("xg", "mx", "pf", "pv", "pd")]
    cp(A(cu), ind(A("nbw"), A(of, S[:, 0:8])))
    act(A(fb), ind(A("tfa"), A(of, S[:, 8:16])))
    act(A(tb), ind(A("tfb"), A(of, S[:, 8:16])))
    for a, b in CH:
        act(A(xg, S[:, 16 * a:16 * b]), ind(A("xw"), A(cu, S[:, a:b])))
    ts(A(c16), A(cu), 2048.0, "subtract")
    for kk in range(4):
        mm(A(pf, S[:, kk:512:4]), A("ibf"), A(fb))
    key = A(pd, S[:, 640:768])
    mm(key, A(c16), A("ibf"), True, False)
    mm(key, A(tb), A("rk"), False, True)
    act(A("key%d" % s), key)
    n = min(m, 5)
    for a, b in ((0, min(n, 4) * 128), (512, 640))[:1 + n // 5]:
        mm(A(pd, S[:, a:b]), A("v16%d" % s), A("e5", S[:, a:b]), True, False)
        mm(A(pd, S[:, a:b]), A(c16), A("ni5", S[:, a:b]), False, True)
    ts(A("eq%d" % s, S[:, 0:n * 128]), A(pd, S[:, 0:n * 128]), 0.0, "is_equal")
    val = A(pv, S[:, 0:128])
    mm(val, A(tb), A("rt"), True, False)
    mm(val, A(fb), A("rf"), False, False)
    for i in range(n):
        mm(val, A("inb"), A("eq%d" % s, S[:, i * 128:(i + 1) * 128]), False, False)
    for a, b in CH:
        for qd in range(4):
            tt(A(mx, S[:, 512 * qd + 4 * a:512 * qd + 4 * b]), A(xg, S[:, 16 * a + qd:16 * b:4]), A(pf, S[:, 4 * a:4 * b]), "max")
    for k in range(16):
        mm(A(pv, S[:, k:128:16]), A(xg, S[:, k:2048:16]), A("r8", S[:, 0:8]), False, False)
    for k in [4 * j + q for q in range(4) for j in range(4)]:
        mm(A(pv, S[:, k:128:16]), A(mx, S[:, 512 * (k % 4) + k // 4:512 * (k % 4) + 512:4]), A("r8", S[:, 8:16]), False, k == 15)
    ns = NSLOT[m]
    P, O, w = "P%s%d" % (POOL[m], s), "O%d%d" % (ns, s), pw(ns)
    for h in (0, 1):
        tt(A(P, S[:, :, h * w + 1:h * w + 17]), A("key%d" % s, S[:, 64 * h:64 * h + 64]), A(pv, S[:, 64 * h:64 * h + 64]), "min")
    for j in range(4):
        scan(A(O, S[:, j, :]), A("keep%d" % ns), A(P, S[:, j, :]), 0.0, "mult", "max")
    B = A(pd, S[:, 768:896])
    for h in (0, 1):
        cp(A("br%d" % s, S[:, 64 * h:64 * h + 64]), A(O, S[:, :, h * w + w - 16:h * w + w]))
    tr(B, A("br%d" % s), A("i32"))
    if m < 6:
        state(s, B, A("st%d" % s), 0)
        if m == 5:
            ts(A("al%d" % s), B, 2.0, "mult", 2 * A18 + TOP, "min")
            ts(A("r1%d" % s), B, 5 * A18 - 4096, "is_ge", 5 * A18 + TOP, "mult")
            tt(A("al%d" % s), A("al%d" % s), A("r1%d" % s), "max")
        to_w(A(pf, S[:, 0:8]), "zmp", lambda a: A("v16%d" % s, S[:, a:128:16]))
        cp(A(of, S[:, 0:8]), A(pf, S[:, 0:8]))
        to_w(A(pd, S[:, 904:912]), "zfi", lambda a: A("v16%d" % s, S[:, a:128:16]))
        cp(A(of, S[:, 8:16]), A(pd, S[:, 904:912]))
        k, w2 = 16 * (NSLOT[m + 1] - 1), pw(NSLOT[m + 1])
        for h in (0, 1):
            tt(A("P%s%d" % (POOL[m + 1], s), S[:, :, h * w2 + 17:h * w2 + 17 + k]), A(P, S[:, :, h * w + 1:h * w + 1 + k]),
               A(O, S[:, :, h * w:h * w + k]), "min")
        return
    ts(A("r1%d" % s), B, 4 * A18 - 4096, "is_ge", 2.0 ** 22, "mult")
    tt(A("r1%d" % s), A("r1%d" % s), B, "min")
    tt(val, A("r1%d" % s), A("al%d" % s), "max")
    half = S[:, 128 * s:128 * s + 128]
    ts(A("flm", half), val, 5 * A18 - 4096, "is_lt", -1.0, "mult")
    ts(A("fl", half), val, 5 * A18 - 4096, "is_ge")
    state(s, val, A("st%d" % s), 1 + rnd)
    if rnd == 0:
        to_w(A(pd, S[:, 896:904]), "zall", lambda a: A("v16%d" % s, S[:, a:128:16]))
        ts(A(of, S[:, 24:32]), A(pd, S[:, 896:904]), 2048.0, "add")
    else:
        ts(A("r1%d" % s), val, A("pf", S[:, 4:5]), "is_ge")
        ts(A("al%d" % s), A("sca", half), 2049.0, "add")
        tt(A("al%d" % s), A("al%d" % s), A("r1%d" % s), "mult")
        ts(A("ymt", half), A("al%d" % s), 1.0, "subtract")


def commit(rnd):
    cnt = A("pf0", S[:, 0:256])
    scan(cnt, A("ones"), A("flm"), -256.0, "mult", "add")
    tt(A("cn16"), cnt, A("fl"), "mult")
    w = A("pd0", S[:, 0:16])
    mm(w, A("ibf"), A("lw16"), True, False)
    to_w(w, "z0", lambda a: A("cn16", S[:, a:256:16]), False)
    cp(A("oc", S[:, 0:16]), w)
    scale(A("sv", S[:, 0:64]), A("ones", S[:, 0:64]), col("pre"))
    cp(ind(A("sv"), A("oc", S[:, 0:16])), A("sca"))
    cp(A("sv16"), A("sv", S[:, 0:64]))
    for i in range(6):
        mm(A("pf0", S[:, i:384:6]), A("rm", S[:, i, :]), A("sv16"))
    cp(A("r16"), A("pf0", S[:, 0:384]))
    wo, wq = A("pd1", S[:, 0:24]), A("pd1", S[:, 512:516])
    for i in range(6):
        mm(A("pv1", S[:, 64 * POS[i]:64 * POS[i] + 64]), A("rm", S[:, i, :]), A("sv16"))
    cp(A("r16b"), A("pv1", S[:, 0:384]))
    to_w(wo, "z0", lambda a: A("r16b", S[:, a:384:16]))
    to_w(wq, "z15", lambda a: A("sv16", S[:, a:64:16]))
    act(A("ws"), wo)
    ts(A("vv"), A("ws"), 2048.0, "add")
    tt(A("vp"), A("vv"), A("dumt"), "min")
    cp(A("oc", S[:, 16:40]), A("vp"))
    act(A("wq"), wq)
    for b in range(4):
        ts(A("oc", S[:, 40 + b:64:4]), A("i6"), A("wq", S[:, b:b + 1]), "add")
    for b in range(3 - 3 * rnd):
        cp(A("oc", S[:, 64 + 4 * b:68 + 4 * b]), A("wq"))
    act(A("chq"), ind(A("chw"), A("oc", S[:, 40:64])))
    act(A("xq"), ind(A("xw"), A("oc", S[:, 16:40])))
    if rnd == 0:
        act(A("hq"), ind(A("sww"), A("oc", S[:, 64:76])))
    pc = "pf1"
    mm(A(pc, S[:, 0:384]), A("ibf"), A("thc"), True, False)
    e0 = 0
    for b in range(4):
        for i in range(6):
            n = 384 - 96 * b
            ts(A("eqc", S[:, e0:e0 + n]), A("r16", S[:, 16 * b:64, :]), A("ws", S[:, 4 * i + b:4 * i + b + 1]), "is_equal")
            mm(A(pc, S[:, 96 * b:96 * b + 96]), A("w2"), A("eqc", S[:, e0:e0 + 96]), False, b == 3 and i == 5)
            if b < 3:
                mm(A(pc, S[:, 96 * b + 96:384]), A("w16"), A("eqc", S[:, e0 + 96:e0 + n]), False, False)
            e0 += n
    ts(A("cf"), A(pc, S[:, 0:384]), 0.0, "is_ge")
    cn = A("pv0", S[:, 0:64])
    mm(cn, A("rmn"), A("sv16"), True, False)
    for i in range(6):
        mm(cn, A("ibf"), A("cf", S[:, i:384:6]), False, i == 5)
    ts(A("ng"), cn, 0.0, "is_ge", 8192.0, "mult")
    ts(A("go"), cn, 0.0, "is_lt", 255.0, "mult")
    to_w(A("pv1", S[:, 0:4]), "z0", lambda a: A("ng", S[:, a:64:16]))
    s1, s2 = A("pd0", S[:, 0:384]), A("pd0", S[:, 512:896])
    mm(s1, A("ibf"), A("xq"), True, False)
    mm(s1, A("ibf"), A("chq"), False, True)
    scale(A("sg"), s1, A("pf", S[:, 7:8]), "sign")
    mm(s2, A("ibf"), A("xq"), True, False)
    mm(s2, A("ibf"), A("chq"), False, False)
    mm(s2, A("i128"), A("sg"), False, True)
    scale(A("new"), s2, A("pf", S[:, 8:9]), "bias")
    tt(A("z3"), A("new", S[:, 0:192]), A("new", S[:, 192:384]), "max")
    tt(A("z2"), A("z3", S[:, 0:64]), A("z3", S[:, 64:128]), "max")
    tt(A("z2"), A("z2"), A("z3", S[:, 128:192]), "max")
    tt(A("zz%d" % rnd), A("z2"), A("go"), "min")
    add("g", "send", A("snt%d" % rnd), [A("zz%d" % rnd)], 0.3, lat=4.0, rnd=rnd)
    for b in range(4):
        ts(A("vp", S[:, b:24:4]), A("vv", S[:, b:24:4]), A("pv1", S[:, b:b + 1]), "add")
    tt(A("vv"), A("vp"), A("dumt"), "min")
    cp(A("oc", S[:, 76:100]), A("vv"))
    if rnd == 0:
        cp(A("nq"), ind(A("nbw"), A("oc", S[:, 16:40])))
        tt(A("nd"), A("nq", S[:, 192:384]), A("nq", S[:, 0:192]), "subtract")
        tt(A("nd"), A("nd"), A("hq"), "mult")
        tt(A("nn", S[:, 0:192]), A("nq", S[:, 0:192]), A("nd"), "add")
        tt(A("nn", S[:, 192:384]), A("nq", S[:, 192:384]), A("nd"), "subtract")
    cp(ind(A("xw"), A("oc", S[:, 76:100])), A("new"))
    if rnd == 0:
        cp(ind(A("nbw"), A("oc", S[:, 76:100])), A("nn"))


def unpack(rnd, out):
    add("v", "recv", A("land%d" % rnd), [A("snt%d" % rnd)], 0.01, rnd=rnd)
    for k in range(3):
        cp(A(out, S[:, k:64:3]), A("land%d" % rnd, S[:, k, k:64:3]))


def lanes(s):
    xs, of, ui = "xs%d" % s, "of%d" % s, "ui%d" % s
    if s == 0:
        unpack(0, xs)
        act(A(xs, S[:, 64:128]), ind(A("xw"), A(of, S[:, 28:32])))
    else:
        act(A(xs), ind(A("xw"), A(of, S[:, 24:32])))
    w = A("pd%d" % s, S[:, 896:904])
    to_w(w, "zw", lambda a: A(xs, S[:, a:128:16]))
    u = [A(ui, S[:, 8 * k:8 * k + 8]) for k in range(6)]
    lw = A("lw", S[:, 8 * s:8 * s + 8])
    cp(u[0], w)
    ts(u[1], u[0], 4095, "bitwise_and")
    ts(u[2], u[1], 37.0, "mult")
    tt(u[3], u[1], u[1], "mult")
    tt(u[2], u[2], lw, "add")
    ts(u[4], u[3], 5, "arith_shift_right", 127, "bitwise_and")
    ts(A("m0w%d" % s), u[2], 4095, "bitwise_and")
    tt(u[5], u[4], lw, "add")
    ts(A("qw%d" % s), u[5], 127, "bitwise_and")


SCRATCH, PACK = {}, {}
ALONE = ("xw", "nbw", "tfa", "chw", "sww", "pari", "wti", "bt", "zz0", "zz1", "ymt", "yzt")


def declare():
    def sb(name, shape, dt):
        LOG[name] = ("sbuf", [128] + list(shape), dt)
    for n in ("pf0", "pf1", "pv0", "pv1"):
        LOG[n] = ("psum", [128, 512], F32)
    for n in ("pd0", "pd1"):
        LOG[n] = ("psum", [128, 1024], F32)
    nc = 16 * len(CN)
    for name, shape, dt in (
            ("xw", [NV + 384], BF), ("nbw", [NV + 384], I32), ("tfa", [768], BF), ("tfb", [768], BF), ("chw", [768], BF),
            ("sww", [128], BF), ("pari", [128], I32), ("wti", [4], I32), ("wtf32", [4], F32), ("bt", [512], I32),
            ("bt16", [512], F16), ("pi", [4], I32), ("pf", [12], F32), ("n144", [144], F32), ("z8f", [144], F32),
            ("nmp", [128], F32), ("n16", [128], F32), ("kpat", [128], F32), ("z8", [144], BF), ("half", [16], F32),
            ("zero", [16], F32), ("kp2", [128], F32), ("wv", [nc], F32), ("wc", [nc], F32), ("r16s", [nc], F32),
            ("ohr", [nc], F32), ("zf", [144], F32), ("bo", [128], F32), ("wq", [4], F32), ("i128", [128], BF),
            ("oh", [16], F32), ("ibf", [128], BF), ("i32", [128], F32), ("inb", [128], BF), ("sg", [384], BF),
            ("ish", [128], BF), ("ni5", [640], BF), ("e5", [640], BF), ("rm", [16, 128], BF), ("rmn", [128], BF),
            ("zmp", [144], BF), ("zfi", [144], BF), ("z0", [144], BF), ("z15", [144], BF), ("zall", [144], BF),
            ("zw", [144], BF), ("rt", [128], BF), ("rf", [128], BF), ("r8", [16], BF), ("rk", [128], BF),
            ("w2", [128], BF), ("w16", [128], BF), ("hli", [256], I32), ("hl", [256], BF), ("ones", [256], F32),
            ("zs", [5, 144], BF), ("ptab", [128], F32), ("stab", [128], F32), ("lw", [16], I32), ("lw16", [16], F16),
            ("dumt", [24], F32), ("i6", [6], F32), ("thc", [64, 6], BF), ("sca", [256], F32), ("fl", [256], F32),
            ("flm", [256], F32), ("ymt", [256], F32), ("cn16", [256], F16), ("oc", [100], U16),
            ("sv", [512], F32), ("sv16", [64], F16), ("r16", [64, 6], F16), ("ws", [24], F32), ("vv", [24], F32),
            ("vp", [24], F32), ("chq", [384], BF), ("xq", [384], BF), ("hq", [192], F32), ("eqc", [5760], BF),
            ("cf", [384], BF), ("ng", [64], BF), ("go", [64], BF), ("new", [384], BF), ("z3", [192], BF),
            ("r16b", [384], F16), ("z2", [64], BF), ("nq", [384], F32), ("nd", [192], F32), ("nn", [384], F32),
            ("yzt", [64], BF)):
        sb(name, shape, dt)
    for n in (1, 2, 3, 4):
        sb("keep%d" % n, [2 * pw(n)], F32)
    for s in (0, 1):
        for name, shape, dt in (
                ("of", [32], U16), ("cu", [128], U16), ("c16", [128], F16), ("fb", [128], BF), ("tb", [128], BF),
                ("xg", [2048], BF), ("mx", [2048], BF), ("eq", [640], BF), ("br", [128], F32),
                ("key", [128], F32), ("st", [128], F32), ("r1", [128], F32), ("l2", [128], F32), ("si", [128], F32),
                ("al", [128], F32), ("v16", [128], F16), ("m0w", [8], I32), ("qw", [8], I32),
                ("m16", [8], F16), ("xs", [128], BF), ("ui", [48], I32), ("zz", [64], BF), ("land", [3, 64], BF)):
            sb("%s%d" % (name, s), shape, dt)
        for m in range(1, 6):
            sb("P%s%d" % (POOL[m], s), [4, 2 * pw(NSLOT[m])], F32)
        for n in (1, 2, 3, 4):
            sb("O%d%d" % (n, s), [4, 2 * pw(n)], F32)
    fillup = {}
    for name, (where, shape, dt) in LOG.items():
        if where == "sbuf" and len(shape) == 2 and name not in ALONE:
            PACK[name] = ("pk" + dt, fillup.get(dt, 0))
            fillup[dt] = fillup.get(dt, 0) + -(-shape[1] // 16) * 16
        else:
            SCRATCH[name] = (where, shape, dt)
    for dt, n in fillup.items():
        SCRATCH["pk" + dt] = ("sbuf", [128, n], dt)


def place(name, idx):
    if name not in PACK:
        return name, idx
    pk, o = PACK[name]
    n = LOG[name][1][1]
    if not isinstance(idx, tuple):
        return pk, (idx, slice(o, o + n))
    a, b, st = idx[1].indices(n)
    return pk, (idx[0], slice(o + a, o + b, st) if st != 1 else slice(o + a, o + b))


def program():
    setup()
    group("b")
    for s in (0, 1):
        begin(s)
    for rnd in (0, 1):
        for m in range(1, 7):
            for s in ((0, 1) if rnd == 0 else (1, 0)):
                group("t")
                turn(rnd, m, s)
        group("c")
        if rnd == 1:
            for gi in range(8):
                dma("y", A("ym", S[gi]), A("ymt", S[16 * gi:16 * gi + 6, :]), 6144)
        commit(rnd)
        if rnd == 0:
            for s in (1, 0):
                group("b")
                lanes(s)
                begin(s)
    dma("s", A("yx"), A("xw", S[:, 0:1024]), 2 ** 18)
    unpack(1, "yzt")
    dma("y", A("yz"), A("yzt"), 16384)


def depend():
    hist, bank = {}, {}
    for i, o in enumerate(OPS):
        dep = {}
        for sp, wr in [(a, False) for a in o["r"]] + [(a, True) for a in o["w"]]:
            where, name, lo, hi = sp[:4]
            if where == "dram" and not name.startswith("snt"):
                continue
            h = hist.setdefault(name, [])
            for j, l2, h2, w2, m2 in h:
                same = o["eng"] == OPS[j]["eng"]
                if j != i and (wr or w2) and l2 < hi and lo < h2 and not (same and (o["eng"] == "t" or not m2 & sp[5])):
                    dep[j] = True
            if wr:
                h[:] = [e for e in h if e[4] & ~sp[5]]
            h.append((i, lo, hi, wr, sp[5]))
            if where == "psum":
                for bk in range(lo // 2048, (hi - 1) // 2048 + 1):
                    e = bank.setdefault((name, bk), [None, [], []])
                    if e[0] != o["eng"]:
                        e[:] = [o["eng"], [], e[1]]
                    for j in e[2]:
                        dep[j] = True
                    if o["eng"] == "t" and e[1] and e[1][-1] != i:
                        dep.setdefault(e[1][-1], False)
                    e[1].append(i)
        o["dep"] = dep


def schedule(lat=0.12, wg=WG, off=OFF):
    n = len(OPS)
    succ = [[] for i in range(n)]
    for i, o in enumerate(OPS):
        for j, hard in o["dep"].items():
            succ[j].append((i, lat if hard else 0.0))
    prio = [0.0] * n
    for i in range(n - 1, -1, -1):
        o = OPS[i]
        prio[i] = o["cost"] + o.get("lat", 0.0) + max([prio[k] + d for k, d in succ[i]] + [0.0])
    for i, o in enumerate(OPS):
        late = o["grp"] if o["eng"] == "t" else min([OPS[k]["grp"] for k, d in succ[i]] + [99])
        prio[i] += off.get(o["cls"], 0.0) - wg * late - 1e-7 * i
    left = [len(o["dep"]) for o in OPS]
    ready_at = [0.0] * n
    free = {e: 0.0 for e in "gtvsy"}
    ready = {e: [] for e in free}
    for i in range(n):
        if not left[i]:
            ready[OPS[i]["eng"]].append(i)
    order = {e: [] for e in free}
    end = 0.0
    for step in range(n):
        t, e = min((max(free[e], min([ready_at[i] for i in ready[e]])), e) for e in free if ready[e])
        i = max([k for k in ready[e] if ready_at[k] <= t], key=lambda k: prio[k])
        ready[e].remove(i)
        order[e].append(i)
        o = OPS[i]
        o["t0"] = t
        free[e] = t + o["cost"]
        done = free[e] + o.get("lat", 0.0)
        end = max(end, done)
        for k, d in succ[i]:
            ready_at[k] = max(ready_at[k], done + d)
            left[k] -= 1
            if not left[k]:
                ready[OPS[k]["eng"]].append(k)
    return order, end


def signals(order):
    needed = set(j for o in OPS for j, hard in o["dep"].items() if hard)
    sig, total = {}, {}
    for e in order:
        for i in order[e]:
            k = OPS[i]["kind"]
            if k == "dma":
                sig[i] = ("d%d" % i, 16, 16)
            elif k in ("send", "recv") or i not in needed:
                continue
            else:
                sig[i] = ("q" + e, total.get("q" + e, 0) + 1, 1)
            total[sig[i][0]] = sig[i][1]
    return sig, total


declare()
program()
depend()
ORDER, ESTIMATE = schedule()
SIG, TOTAL = signals(ORDER)
SEMAPHORES = sorted(TOTAL) + ["arr0", "arr1", "sent"]
ALU = {"add": AluOpType.add, "subtract": AluOpType.subtract, "mult": AluOpType.mult, "max": AluOpType.max,
       "min": AluOpType.min, "is_ge": AluOpType.is_ge, "is_lt": AluOpType.is_lt, "is_equal": AluOpType.is_equal,
       "not_equal": AluOpType.not_equal, "bitwise_and": AluOpType.bitwise_and,
       "arith_shift_right": AluOpType.arith_shift_right}


def masks(topo, src, dsts):
    used, out = set(), {}
    for d in sorted(dsts, key=lambda d: len(topo.engines(src, d))):
        out[d] = [k for k in topo.engines(src, d) if k not in used][:4]
        used.update(out[d])
    return out


def rank_program(g, core, T, topo):
    rank = T.rank_of(core)
    if rank is None:
        return
    cores = list(T.cores)
    n = len(cores)
    plan = {c: masks(topo, c, [d for d in cores if d != c]) for c in cores}
    arrive = sum(len(plan[c][core]) for c in cores if c != core)
    queue = {"g": g, "t": g.tensor, "v": g.vector, "s": g.scalar, "y": g.sync}

    def R(a):
        if not isinstance(a, tuple):
            return a
        if a[0] == "ind":
            return R(a[1]).indirect(R(a[2]))
        name, idx = place(a[1], a[2])
        return T[name][idx]

    sent = [0]
    seen = {e: {} for e in queue}

    def wait(e, sem, val):
        if seen[e].get(sem, 0) < val:
            seen[e][sem] = val
            queue[e].wait_ge(T.sem[sem], val)

    def emit(i):
        o = OPS[i]
        e, k = o["eng"], o["kind"]
        q = queue[e]
        need = {}
        for j, hard in o["dep"].items():
            if hard and j in SIG:
                need[SIG[j][0]] = max(need.get(SIG[j][0], 0), SIG[j][1])
        for sem in sorted(need):
            wait(e, sem, need[sem])
        if k == "recv":
            wait(e, "arr%d" % o["rnd"], arrive)
            return
        if k == "send":
            tf = []
            for d in range(3):
                dst = cores[(rank + 1 + d) % n]
                rid, pid = topo.addr(dst)[:2]
                tf.append(RemoteDMATransfer(dst_ids=[DstId(rid=rid, pnc=pid)], dma_engine_mask=sum(1 << x for x in plan[core][dst]),
                                            remote_sem=T.sem["arr%d" % o["rnd"]], src=T["zz%d" % o["rnd"]][:],
                                            dst=T["land%d" % o["rnd"]][:, d, :]))
                sent[0] += len(plan[core][dst])
            g.remote_dma_fused(tf, local_sem=T.sem.sent)
            return
        a = [R(x) for x in o["ins"]]
        out = R(o["out"])
        if k == "mm":
            c = q.matmul(out, a[0], a[1], o["start"], o["stop"])
        elif k == "tr":
            c = q.transpose(out, a[0], a[1])
        elif k == "cp":
            c = q.tensor_copy(out, a[0])
        elif k == "tt":
            c = q.tensor_tensor(out, a[0], a[1], ALU[o["op"]])
        elif k == "ts" and o["op1"] is None:
            c = q.tensor_scalar(out, a[0], a[1], None, ALU[o["op0"]])
        elif k == "ts":
            c = q.tensor_scalar(out, a[0], a[1], a[2], ALU[o["op0"]], ALU[o["op1"]])
        elif k == "scan":
            c = q.tensor_tensor_scan(out, a[0], a[1], a[2], ALU[o["op0"]], ALU[o["op1"]])
        elif k == "ms":
            c = q.memset(out, o["val"])
        elif k == "act" and len(a) > 1:
            c = q.activation(out, a[0], ActivationFunctionType.Identity, scale=a[1])
        elif k == "act":
            c = q.activation(out, a[0], ActivationFunctionType.Identity)
        elif k == "sign":
            c = q.activation(out, a[0], ActivationFunctionType.Sign, bias=a[1])
        elif k == "bias":
            c = q.activation(out, a[0], ActivationFunctionType.Identity, bias=a[1])
        elif k == "iota" and info(o["out"][1])[2] == I32:
            c = q.iota(out, o["pattern"], o["base"], o["cm"])
        elif k == "iota":
            c = q.iota(out, o["pattern"], o["base"], o["cm"], allow_small_or_imprecise_dtypes=True)
        else:
            c = q.dma_start(out, a[0])
        if i in SIG:
            c.then_inc(T.sem[SIG[i][0]], SIG[i][2])

    for i in sorted(range(len(OPS)), key=lambda i: (OPS[i]["t0"], i)):
        emit(i)
    for sem in sorted(TOTAL):
        wait("g", sem, TOTAL[sem])
    wait("g", "sent", sent[0])
